import numpy as np
import ml_dtypes


def mxq(x, axis, fmt="e4m3"):
    dtype, down = {"e4m3": (ml_dtypes.float8_e4m3fn, 7), "e5m2": (ml_dtypes.float8_e5m2, 14)}[fmt]
    v = np.moveaxis(np.asarray(x, np.float32).astype(ml_dtypes.bfloat16).astype(np.float64), axis, -1)
    blocks = v.reshape(v.shape[:-1] + (-1, 32))
    amax = np.abs(blocks).max(-1, keepdims=True)
    byte = np.maximum(np.where(amax > 0, np.frexp(amax)[1] - 1 + 127, 0) - down, 1)
    scale = np.exp2(byte - 127.0)
    codes = (blocks / scale).astype(np.float32).astype(dtype).astype(np.float64)
    return np.moveaxis((codes * scale).reshape(v.shape), -1, axis)


WIDE = False


def mx_kscale(k):
    if not WIDE:
        return np.ones(k)
    levels = np.array([30, -30])
    if k % 512:
        return np.exp2(np.random.permutation(np.resize(levels, k // 32))).repeat(32)
    a = np.empty((k // 512, 16))
    for p in range(k // 512):
        a[p, :8] = np.random.permutation(np.resize(levels, 8))
        for g in range(8):
            far = levels[np.abs(levels - a[p, g]) >= 10]
            a[p, g + 8] = far[np.random.randint(len(far))]
    return np.exp2(a.ravel()).repeat(32)


def f64(x):
    return np.asarray(x).astype(np.float64)


def striped(idx):
    return np.tile(np.asarray(idx).reshape(-1, 16).T, (8, 1)).astype(np.uint16)


def unstriped(offs):
    return offs[:16].T.reshape(-1).astype(np.int64)


E2M1 = np.array([0.0, 0.5, 1.0, 1.5, 2.0, 3.0, 4.0, 6.0, -0.0, -0.5, -1.0, -1.5, -2.0, -3.0, -4.0, -6.0])


def pack_weight(w, fmt):
    k, n = w.shape
    w = f64(np.asarray(w, np.float32).astype(ml_dtypes.bfloat16)).reshape(k // 32, 32, n)
    amax = np.abs(w).max(1)
    if fmt in ("e4m3", "e5m2"):
        byte = np.frexp(amax)[1] - 1 + 127 - (7 if fmt == "e4m3" else 14)
    else:
        mant, ex = np.frexp(amax / 6.0)
        byte = np.where(mant > 0.5, ex, ex - 1) + 127
    byte = np.clip(np.where(amax > 0, byte, 1), 1, 254)
    scaled = (w * np.exp2(127.0 - byte)[:, None, :]).reshape(k, n).astype(np.float32)
    by_word = np.ascontiguousarray(scaled.reshape(k // 512, 128, 4, n).transpose(0, 1, 3, 2))
    if fmt in ("e4m3", "e5m2"):
        words = by_word.astype(ml_dtypes.float8_e4m3fn if fmt == "e4m3" else ml_dtypes.float8_e5m2).view(np.uint8)
    else:
        c = by_word.astype(ml_dtypes.float4_e2m1fn).view(np.uint8) & 0xF
        words = (c[..., 0::2] | (c[..., 1::2] << 4)).reshape(k // 512, 128, 2 * n)
    return np.ascontiguousarray(words), np.ascontiguousarray(byte.astype(np.uint8).reshape(k // 512, 16, n))


def unpack_weight(words, scales, fmt):
    g, _, n = scales.shape
    words = np.ascontiguousarray(words).reshape(g, 128, n, -1)
    if fmt in ("e4m3", "e5m2"):
        vals = words.view(ml_dtypes.float8_e4m3fn if fmt == "e4m3" else ml_dtypes.float8_e5m2).astype(np.float64)
    else:
        nib = np.empty((g, 128, n, 4), np.uint8)
        nib[..., 0::2] = words & 0xF
        nib[..., 1::2] = words >> 4
        vals = E2M1[nib]
    vals = vals * np.repeat(np.exp2(scales.astype(np.float64) - 127.0), 8, axis=1)[..., None]
    return vals.transpose(0, 1, 3, 2).reshape(g * 512, n)


def sigmoid(v):
    return 1.0 / (1.0 + np.exp(-v))


def sgn(shape):
    return np.random.uniform(0.5, 2.0, shape) * np.where(np.random.standard_normal(shape) < 0, -1.0, 1.0)


K, T, J, R, F, Z, N, C, O = 512, 1024, 256, 512, 512, 1024, 256, 512, 128


def setup_inputs():
    n = np.random.standard_normal
    idx = np.random.permutation(T)[:J]
    idx2 = np.random.permutation(Z)[:J]
    idx3 = np.random.permutation(C)[:J]
    idx4 = np.random.permutation(C)[:O]
    idx5 = np.random.permutation(C)[:O]
    idx6 = np.random.permutation(J)[:O]
    fk = mx_kscale(K)
    ff = mx_kscale(F)
    fr = mx_kscale(R)
    xtp = pack_weight(n((K, T)) / fk[:, None], "e4m3")
    xop = pack_weight(n((F, Z)) / ff[:, None], "e2m1")
    wp = pack_weight(n((K, R)) * 1 / np.sqrt(K) * fk[:, None] * fr, "e2m1")
    w0p = pack_weight(n((F, R)) * 1 / np.sqrt(F) * ff[:, None] * fr, "e5m2")
    w2p = pack_weight(n((F, R)) * 1 / np.sqrt(F) * ff[:, None] * fr, "e5m2")
    wbp = pack_weight(n((R, N)) * 1 / np.sqrt(R) / fr[:, None], "e5m2")
    wcp = pack_weight(n((R, N)) * 1 / np.sqrt(R) / fr[:, None], "e2m1")
    return {
        "xt_words": xtp[0],
        "xt_scales": xtp[1],
        "xo_words": xop[0],
        "xo_scales": xop[1],
        "w_words": wp[0],
        "w_scales": wp[1],
        "w0_words": w0p[0],
        "w0_scales": w0p[1],
        "w2_words": w2p[0],
        "w2_scales": w2p[1],
        "wb_words": wbp[0],
        "wb_scales": wbp[1],
        "wc_words": wcp[0],
        "wc_scales": wcp[1],
        "so": (np.random.uniform(0.5, 1.6, (N, 1))).astype(np.float32),
        "sp": (sgn((N, 1))).astype(np.float32),
        "bo": (np.random.uniform(-2.0, 2.0, (N, 1))).astype(np.float32),
        "offs": striped(idx),
        "offs2": striped(idx2),
        "offs3": striped(idx3),
        "offs4": striped(idx4),
        "offs5": striped(idx5),
        "offs6": striped(idx6),
    }


def reference(xt_words, xt_scales, xo_words, xo_scales, w_words, w_scales, w0_words, w0_scales, w2_words, w2_scales, wb_words, wb_scales, wc_words, wc_scales, so, sp, bo, offs, offs2, offs3, offs4, offs5, offs6):
    idx = unstriped(offs)
    idx2 = unstriped(offs2)
    idx3 = unstriped(offs3)
    idx4 = unstriped(offs4)
    idx5 = unstriped(offs5)
    idx6 = unstriped(offs6)
    xtu = unpack_weight(xt_words, xt_scales, "e4m3")
    xou = unpack_weight(xo_words, xo_scales, "e2m1")
    wu = unpack_weight(w_words, w_scales, "e2m1")
    w0u = unpack_weight(w0_words, w0_scales, "e5m2")
    w2u = unpack_weight(w2_words, w2_scales, "e5m2")
    wbu = unpack_weight(wb_words, wb_scales, "e5m2")
    wcu = unpack_weight(wc_words, wc_scales, "e2m1")
    xtidxg = xtu[:, idx]
    xoidx2g = xou[:, idx2]
    a = wu.T @ xtidxg + w0u.T @ xoidx2g
    b = w2u.T @ xoidx2g
    hid = np.abs(a - b)
    hidq = mxq(hid, 0, "e4m3")
    p = wbu.T @ hidq
    q = wcu.T @ hidq
    pw = np.zeros((N, C))
    pw[:, idx3] = p
    y = pw[:, idx4] * f64(so) * sigmoid(pw[:, idx5] * f64(sp) + f64(bo)) - q[:, idx6]
    return y

@@ -1,0 +1,223 @@
+from contextlib import ExitStack
+
+import concourse.mybir as mybir
+from concourse.masks import make_identity
+
+FLOPS = 536870912
+
+F32 = mybir.dt.float32
+BF16 = mybir.dt.bfloat16
+I32 = mybir.dt.int32
+U32 = mybir.dt.uint32
+U16 = mybir.dt.uint16
+U8 = mybir.dt.uint8
+E4M3 = mybir.dt.float8_e4m3fn_x4
+E5M2 = mybir.dt.float8_e5m2_x4
+E2M1 = mybir.dt.float4_e2m1fn_x4
+ACT = mybir.ActivationFunctionType
+ALU = mybir.AluOpType
+
+P = 128
+T = 1024
+J = 256
+R = 512
+N = 256
+C = 512
+O = 128
+HALVES = J // P
+TILES = N // P
+LIST_COLS = P // 16
+
+
+def tile_list_outcomegatedboard_noted_kernel(
+    tc, xt_words, xt_scales, xo_words, xo_scales, w_words, w_scales, w0_words, w0_scales,
+    w2_words, w2_scales, wb_words, wb_scales, wc_words, wc_scales, so, sp, bo,
+    offs, offs2, offs3, offs4, offs5, offs6, out,
+):
+    nc = tc.nc
+    with ExitStack() as ctx:
+        keep = ctx.enter_context(tc.tile_pool(name="keep", bufs=1))
+        psum = ctx.enter_context(tc.psum_pool(name="psum", bufs=1))
+
+        def sb(name, shape, dtype, tag=""):
+            return keep.tile(shape, dtype, name=name, tag=tag or name, align_bytes=64)
+
+        def bank(name, tag, shape):
+            return psum.tile(shape, F32, name=name, tag=tag)
+
+        def load_list(name, src):
+            tile = keep.tile(list(src.shape), U16, name=name)
+            nc.sync.dma_start(tile[:], src)
+            return tile
+
+        def load_words(name, src, dtype, columns):
+            rows = src[0]
+            if rows.ndim == 3:
+                rows = rows.rearrange("p c t -> p (c t)")
+            tile = sb(name, [P, columns], dtype)
+            nc.sync.dma_start(tile[:].bitcast(I32), rows.bitcast(I32))
+            return tile
+
+        def zero_plane(name, columns):
+            plane = sb(name, [P, columns], U8)
+            nc.vector.memset(plane[:].bitcast(I32), 0)
+            return plane
+
+        def load_plane(queue, plane, src):
+            by_r = src[0].rearrange("(q r) c -> r q c", r=4)
+            for r in range(4):
+                queue.dma_start(plane[r:P:32, :].bitcast(I32), by_r[r].bitcast(I32))
+
+        def stage_plane(queue, name, src):
+            columns = src.shape[2]
+            stage = sb(name, [4, 4, columns // 4], I32)
+            queue.dma_start(stage[:], src[0].rearrange("(q r) c -> r q c", r=4).bitcast(I32))
+            return stage
+
+        def spread_plane(plane, stage):
+            for q in range(4):
+                nc.vector.tensor_copy(plane[32 * q : 32 * q + 4, :].bitcast(I32), stage[:, q, :])
+
+        def load_column(name, src):
+            tile = sb(name, [P, TILES], F32)
+            with nc.allow_non_contiguous_dma(reason="one value a partition"):
+                nc.sync.dma_start(tile[:], src.rearrange("(n p) o -> p (n o)", p=P))
+            return tile
+
+        xo_s = zero_plane("xo_s", T)
+        xt_s = zero_plane("xt_s", T)
+        w2_s = zero_plane("w2_s", R)
+        w0_s = zero_plane("w0_s", R)
+        w_s = zero_plane("w_s", R)
+        wb_s = zero_plane("wb_s", N)
+        wc_s = zero_plane("wc_s", N)
+        boards = []
+        for n in range(TILES):
+            board = sb("board%d" % n, [P, C], F32)
+            nc.vector.memset(board[:], 0.0)
+            boards.append(board)
+
+        ident = sb("ident", [P, P], F32)
+        make_identity(nc, ident[:])
+
+        xo_w = load_words("xo_w", xo_words, U16, T)
+        xo_stage = stage_plane(nc.scalar, "xo_stage", xo_scales)
+        list2 = load_list("list2", offs2)
+        w2_stage = stage_plane(nc.scalar, "w2_stage", w2_scales)
+        w2_w = load_words("w2_w", w2_words, U32, R)
+        w0_w = load_words("w0_w", w0_words, U32, R)
+        w0_stage = stage_plane(nc.sync, "w0_stage", w0_scales)
+        xt_w = load_words("xt_w", xt_words, U32, T)
+        list1 = load_list("list1", offs)
+        w_stage = stage_plane(nc.sync, "w_stage", w_scales)
+        load_plane(nc.sync, xt_s, xt_scales)
+        w_w = load_words("w_w", w_words, U16, R)
+        wb_w = load_words("wb_w", wb_words, U32, N)
+        load_plane(nc.sync, wb_s, wb_scales)
+        list3 = load_list("list3", offs3)
+        wc_w = load_words("wc_w", wc_words, U16, N)
+        load_plane(nc.sync, wc_s, wc_scales)
+        list6 = load_list("list6", offs6)
+        list4 = load_list("list4", offs4)
+        list5 = load_list("list5", offs5)
+        so_t = load_column("so_t", so)
+        sp_t = load_column("sp_t", sp)
+        bo_t = load_column("bo_t", bo)
+
+        def gather(name, table, dtype, offsets):
+            picked = sb(name, [P, 16 * offsets.shape[1]], dtype)
+            nc.vector.tensor_copy(picked[:], table[:].indirect(offsets))
+            return picked
+
+        def half(lst, h):
+            return lst[:, h * LIST_COLS : (h + 1) * LIST_COLS]
+
+        a_ps = [bank("a%d" % h, "a%d" % h, [P, R]) for h in range(HALVES)]
+        b_sb = []
+        xo_g = []
+        spread_plane(xo_s, xo_stage)
+        for h in range(HALVES):
+            gs = gather("xo_gs%d" % h, xo_s, U8, half(list2, h))
+            gw = gather("xo_gw%d" % h, xo_w, U16, half(list2, h))
+            if h == 0:
+                spread_plane(w2_s, w2_stage)
+            b_ps = bank("b%d" % h, "b%d" % h, [P, R])
+            nc.tensor.matmul_mx(b_ps[:], gw[:].bitcast(E2M1), gs[:], w2_w[:].bitcast(E5M2), w2_s[:], start=True, stop=True)
+            b_h = sb("b_sb%d" % h, [P, 2, P, 2], F32)
+            nc.scalar.copy(b_h[:], b_ps[:].rearrange("j (p u e) -> j u p e", u=2, e=2))
+            b_sb.append(b_h)
+            xo_g.append((gw, gs))
+        spread_plane(w0_s, w0_stage)
+        for h in range(HALVES):
+            gw, gs = xo_g[h]
+            nc.tensor.matmul_mx(a_ps[h][:], gw[:].bitcast(E2M1), gs[:], w0_w[:].bitcast(E5M2), w0_s[:], start=True, stop=False)
+        spread_plane(w_s, w_stage)
+        for h in range(HALVES):
+            gw = gather("xt_gw%d" % h, xt_w, U32, half(list1, h))
+            gs = gather("xt_gs%d" % h, xt_s, U8, half(list1, h))
+            nc.tensor.matmul_mx(
+                a_ps[h][:], gw[:].bitcast(E4M3), gs[:], w_w[:].bitcast(E2M1), w_s[:],
+                start=False, stop=True,
+            )
+
+        turned_ps = []
+        for h in range(HALVES):
+            turned = bank("turned%d" % h, "turned%d" % h, [P, 4, P])
+            a_view = a_ps[h][:].rearrange("j (p u e) -> j u p e", u=2, e=2)
+            for u in range(2):
+                diff = sb("diff%d%d" % (h, u), [P, P, 2], F32)
+                nc.vector.tensor_tensor(diff[:], a_view[:, u], b_sb[h][:, u], ALU.subtract)
+                for e in range(2):
+                    nc.tensor.transpose(turned[:, 2 * u + e, :], diff[:, :, e], ident[:])
+            turned_ps.append(turned)
+
+        hid_w = sb("hid_w", [P, J], U32)
+        hid_s = sb("hid_s", [P, J], U8)
+        for h in range(HALVES):
+            turned = turned_ps[h]
+            hid = sb("hid%d" % h, [P, P, 4], BF16)
+            nc.scalar.activation(hid[:], turned[:].rearrange("p t j -> p j t"), ACT.Abs)
+            cols = slice(h * P, (h + 1) * P)
+            nc.vector.quantize_mx(hid_w[:, cols].bitcast(E4M3), hid_s[:, cols], hid[:].rearrange("p j t -> p (j t)"))
+        for h in range(HALVES):
+            cols = slice(h * P, (h + 1) * P)
+            for n in reversed(range(TILES)):
+                rows = slice(n * P, (n + 1) * P)
+                p_ps = bank("p%d%d" % (h, n), ("p%d" if h == 0 else "b%d") % n, [P, P])
+                nc.tensor.matmul_mx(
+                    p_ps[:], wb_w[:, rows].bitcast(E5M2), wb_s[:, rows], hid_w[:, cols].bitcast(E4M3), hid_s[:, cols],
+                    start=True, stop=True,
+                )
+                p_sb = sb("p_sb%d%d" % (h, n), [P, P], F32, "hid1" if h + n == 0 else "")
+                places = boards[n][:].indirect(half(list3, h))
+                if n == 0:
+                    nc.vector.tensor_copy(p_sb[:], p_ps[:])
+                    nc.vector.tensor_copy(places, p_sb[:])
+                else:
+                    nc.scalar.copy(p_sb[:], p_ps[:])
+                    nc.scalar.activation(places, p_sb[:], ACT.Copy)
+
+        q_g = []
+        for n in range(TILES):
+            rows = slice(n * P, (n + 1) * P)
+            q_ps = bank("q%d" % n, "a%d" % n, [P, J])
+            nc.tensor.matmul_mx(
+                q_ps[:], wc_w[:, rows].bitcast(E2M1), wc_s[:, rows], hid_w[:].bitcast(E4M3), hid_s[:],
+                start=True, stop=True,
+            )
+            q_sb = sb("q_sb%d" % n, [P, J], F32)
+            nc.vector.tensor_copy(q_sb[:], q_ps[:])
+            q_g.append(q_sb)
+
+        for n in reversed(range(TILES)):
+            col = slice(n, n + 1)
+            value = sb("value%d" % n, [P, O], F32)
+            gate = sb("gate%d" % n, [P, O], F32)
+            nc.scalar.activation(value[:], boards[n][:].indirect(list4[:]), ACT.Copy, scale=so_t[:, col])
+            nc.scalar.activation(gate[:], boards[n][:].indirect(list5[:]), ACT.Sigmoid, bias=bo_t[:, col], scale=sp_t[:, col])
+            taken = gather("taken%d" % n, q_g[n], F32, list6[:])
+            gated = sb("gated%d" % n, [P, O], F32)
+            nc.vector.tensor_tensor(gated[:], value[:], gate[:], ALU.mult)
+            result = sb("result%d" % n, [P, O], F32)
+            nc.vector.tensor_tensor(result[:], gated[:], taken[:], ALU.subtract)
+            nc.sync.dma_start(out[n * P : (n + 1) * P, :], result[:])

@@ -97,6 +97,8 @@ def tile_list_outcomegatedboard_noted_kernel(
             nc.vector.memset(board[:], 0.0)
             boards.append(board)
 
+        warm = sb("warm", [P, 1], F32)
+        nc.scalar.activation(warm[:], boards[0][:, 0:1], ACT.Sigmoid)
         ident = sb("ident", [P, P], F32)
         make_identity(nc, ident[:])
 

@@ -58,25 +58,15 @@ def tile_list_outcomegatedboard_noted_kernel(
             nc.sync.dma_start(tile[:].bitcast(I32), rows.bitcast(I32))
             return tile
 
-        def zero_plane(name, columns):
+        def zero_plane(name, columns, engine=nc.vector):
             plane = sb(name, [P, columns], U8)
-            nc.vector.memset(plane[:].bitcast(I32), 0)
+            engine.memset(plane[:].bitcast(I32), 0)
             return plane
 
         def load_plane(queue, plane, src):
             by_r = src[0].rearrange("(q r) c -> r q c", r=4)
             for r in range(4):
                 queue.dma_start(plane[r:P:32, :].bitcast(I32), by_r[r].bitcast(I32))
-
-        def stage_plane(queue, name, src):
-            columns = src.shape[2]
-            stage = sb(name, [4, 4, columns // 4], I32)
-            queue.dma_start(stage[:], src[0].rearrange("(q r) c -> r q c", r=4).bitcast(I32))
-            return stage
-
-        def spread_plane(plane, stage):
-            for q in range(4):
-                nc.vector.tensor_copy(plane[32 * q : 32 * q + 4, :].bitcast(I32), stage[:, q, :])
 
         def load_column(name, src):
             tile = sb(name, [P, TILES], F32)
@@ -85,9 +75,9 @@ def tile_list_outcomegatedboard_noted_kernel(
             return tile
 
         xo_s = zero_plane("xo_s", T)
-        xt_s = zero_plane("xt_s", T)
         w2_s = zero_plane("w2_s", R)
-        w0_s = zero_plane("w0_s", R)
+        xt_s = zero_plane("xt_s", T)
+        w0_s = zero_plane("w0_s", R, nc.gpsimd)
         w_s = zero_plane("w_s", R)
         wb_s = zero_plane("wb_s", N)
         wc_s = zero_plane("wc_s", N)
@@ -97,31 +87,33 @@ def tile_list_outcomegatedboard_noted_kernel(
             nc.vector.memset(board[:], 0.0)
             boards.append(board)
 
-        warm = sb("warm", [P, 1], F32)
-        nc.scalar.activation(warm[:], boards[0][:, 0:1], ACT.Sigmoid)
+        warm_in = sb("warm_in", [P, 1], F32)
+        warm_out = sb("warm_out", [P, 1], F32)
+        nc.vector.memset(warm_in[:], 0.0)
+        nc.scalar.activation(warm_out[:], warm_in[:], ACT.Sigmoid)
+        load_plane(nc.gpsimd, w0_s, w0_scales)
         ident = sb("ident", [P, P], F32)
         make_identity(nc, ident[:])
 
         xo_w = load_words("xo_w", xo_words, U16, T)
-        xo_stage = stage_plane(nc.scalar, "xo_stage", xo_scales)
         list2 = load_list("list2", offs2)
-        w2_stage = stage_plane(nc.scalar, "w2_stage", w2_scales)
+        load_plane(nc.sync, xo_s, xo_scales)
         w2_w = load_words("w2_w", w2_words, U32, R)
-        w0_w = load_words("w0_w", w0_words, U32, R)
-        w0_stage = stage_plane(nc.sync, "w0_stage", w0_scales)
         xt_w = load_words("xt_w", xt_words, U32, T)
+        load_plane(nc.sync, w2_s, w2_scales)
+        w0_w = load_words("w0_w", w0_words, U32, R)
         list1 = load_list("list1", offs)
-        w_stage = stage_plane(nc.sync, "w_stage", w_scales)
         load_plane(nc.sync, xt_s, xt_scales)
         w_w = load_words("w_w", w_words, U16, R)
+        load_plane(nc.sync, w_s, w_scales)
         wb_w = load_words("wb_w", wb_words, U32, N)
         load_plane(nc.sync, wb_s, wb_scales)
         list3 = load_list("list3", offs3)
         wc_w = load_words("wc_w", wc_words, U16, N)
         load_plane(nc.sync, wc_s, wc_scales)
-        list6 = load_list("list6", offs6)
         list4 = load_list("list4", offs4)
         list5 = load_list("list5", offs5)
+        list6 = load_list("list6", offs6)
         so_t = load_column("so_t", so)
         sp_t = load_column("sp_t", sp)
         bo_t = load_column("bo_t", bo)
@@ -137,23 +129,18 @@ def tile_list_outcomegatedboard_noted_kernel(
         a_ps = [bank("a%d" % h, "a%d" % h, [P, R]) for h in range(HALVES)]
         b_sb = []
         xo_g = []
-        spread_plane(xo_s, xo_stage)
         for h in range(HALVES):
             gs = gather("xo_gs%d" % h, xo_s, U8, half(list2, h))
             gw = gather("xo_gw%d" % h, xo_w, U16, half(list2, h))
-            if h == 0:
-                spread_plane(w2_s, w2_stage)
             b_ps = bank("b%d" % h, "b%d" % h, [P, R])
             nc.tensor.matmul_mx(b_ps[:], gw[:].bitcast(E2M1), gs[:], w2_w[:].bitcast(E5M2), w2_s[:], start=True, stop=True)
             b_h = sb("b_sb%d" % h, [P, 2, P, 2], F32)
             nc.scalar.copy(b_h[:], b_ps[:].rearrange("j (p u e) -> j u p e", u=2, e=2))
             b_sb.append(b_h)
             xo_g.append((gw, gs))
-        spread_plane(w0_s, w0_stage)
         for h in range(HALVES):
             gw, gs = xo_g[h]
             nc.tensor.matmul_mx(a_ps[h][:], gw[:].bitcast(E2M1), gs[:], w0_w[:].bitcast(E5M2), w0_s[:], start=True, stop=False)
-        spread_plane(w_s, w_stage)
         for h in range(HALVES):
             gw = gather("xt_gw%d" % h, xt_w, U32, half(list1, h))
             gs = gather("xt_gs%d" % h, xt_s, U8, half(list1, h))

@@ -186,17 +186,15 @@ def tile_list_outcomegatedboard_noted_kernel(
                     nc.scalar.copy(p_sb[:], p_ps[:])
                     nc.scalar.activation(places, p_sb[:], ACT.Copy)
 
-        q_g = []
+        q_ps = bank("q", "a0", [P, TILES, J])
         for n in range(TILES):
             rows = slice(n * P, (n + 1) * P)
-            q_ps = bank("q%d" % n, "a%d" % n, [P, J])
             nc.tensor.matmul_mx(
-                q_ps[:], wc_w[:, rows].bitcast(E2M1), wc_s[:, rows], hid_w[:].bitcast(E4M3), hid_s[:],
+                q_ps[:, n], wc_w[:, rows].bitcast(E2M1), wc_s[:, rows], hid_w[:].bitcast(E4M3), hid_s[:],
                 start=True, stop=True,
             )
-            q_sb = sb("q_sb%d" % n, [P, J], F32)
-            nc.vector.tensor_copy(q_sb[:], q_ps[:])
-            q_g.append(q_sb)
+        q_sb = sb("q_sb", [P, TILES * J], F32)
+        nc.vector.tensor_copy(q_sb[:], q_ps[:].rearrange("p n j -> p (n j)"))
 
         for n in reversed(range(TILES)):
             col = slice(n, n + 1)
@@ -204,9 +202,10 @@ def tile_list_outcomegatedboard_noted_kernel(
             gate = sb("gate%d" % n, [P, O], F32)
             nc.scalar.activation(value[:], boards[n][:].indirect(list4[:]), ACT.Copy, scale=so_t[:, col])
             nc.scalar.activation(gate[:], boards[n][:].indirect(list5[:]), ACT.Sigmoid, bias=bo_t[:, col], scale=sp_t[:, col])
-            taken = gather("taken%d" % n, q_g[n], F32, list6[:])
+            taken = gather("taken%d" % n, q_sb[:, n * J : (n + 1) * J], F32, list6[:])
             gated = sb("gated%d" % n, [P, O], F32)
-            nc.vector.tensor_tensor(gated[:], value[:], gate[:], ALU.mult)
+            multiplier = nc.gpsimd if n == 1 else nc.vector
+            multiplier.tensor_tensor(gated[:], value[:], gate[:], ALU.mult)
             result = sb("result%d" % n, [P, O], F32)
             nc.vector.tensor_tensor(result[:], gated[:], taken[:], ALU.subtract)
             nc.sync.dma_start(out[n * P : (n + 1) * P, :], result[:])

from contextlib import ExitStack

import concourse.mybir as mybir
from concourse.masks import make_identity

FLOPS = 536870912

F32 = mybir.dt.float32
BF16 = mybir.dt.bfloat16
I32 = mybir.dt.int32
U32 = mybir.dt.uint32
U16 = mybir.dt.uint16
U8 = mybir.dt.uint8
E4M3 = mybir.dt.float8_e4m3fn_x4
E5M2 = mybir.dt.float8_e5m2_x4
E2M1 = mybir.dt.float4_e2m1fn_x4
ACT = mybir.ActivationFunctionType
ALU = mybir.AluOpType

P = 128
T = 1024
J = 256
R = 512
N = 256
C = 512
O = 128
HALVES = J // P
TILES = N // P
LIST_COLS = P // 16


def tile_list_outcomegatedboard_noted_kernel(
    tc, xt_words, xt_scales, xo_words, xo_scales, w_words, w_scales, w0_words, w0_scales,
    w2_words, w2_scales, wb_words, wb_scales, wc_words, wc_scales, so, sp, bo,
    offs, offs2, offs3, offs4, offs5, offs6, out,
):
    nc = tc.nc
    with ExitStack() as ctx:
        keep = ctx.enter_context(tc.tile_pool(name="keep", bufs=1))
        psum = ctx.enter_context(tc.psum_pool(name="psum", bufs=1))

        def sb(name, shape, dtype, tag=""):
            return keep.tile(shape, dtype, name=name, tag=tag or name, align_bytes=64)

        def bank(name, tag, shape):
            return psum.tile(shape, F32, name=name, tag=tag)

        def load_list(name, src):
            tile = keep.tile(list(src.shape), U16, name=name)
            nc.sync.dma_start(tile[:], src)
            return tile

        def load_words(name, src, dtype, columns):
            rows = src[0]
            if rows.ndim == 3:
                rows = rows.rearrange("p c t -> p (c t)")
            tile = sb(name, [P, columns], dtype)
            nc.sync.dma_start(tile[:].bitcast(I32), rows.bitcast(I32))
            return tile

        def zero_plane(name, columns, engine=nc.vector):
            plane = sb(name, [P, columns], U8)
            engine.memset(plane[:].bitcast(I32), 0)
            return plane

        def load_plane(queue, plane, src):
            by_r = src[0].rearrange("(q r) c -> r q c", r=4)
            for r in range(4):
                queue.dma_start(plane[r:P:32, :].bitcast(I32), by_r[r].bitcast(I32))

        def load_column(name, src):
            tile = sb(name, [P, TILES], F32)
            with nc.allow_non_contiguous_dma(reason="one value a partition"):
                nc.sync.dma_start(tile[:], src.rearrange("(n p) o -> p (n o)", p=P))
            return tile

        xo_s = zero_plane("xo_s", T)
        w2_s = zero_plane("w2_s", R)
        xt_s = zero_plane("xt_s", T)
        w0_s = zero_plane("w0_s", R, nc.gpsimd)
        w_s = zero_plane("w_s", R)
        wb_s = zero_plane("wb_s", N)
        wc_s = zero_plane("wc_s", N)
        boards = []
        for n in range(TILES):
            board = sb("board%d" % n, [P, C], F32)
            nc.vector.memset(board[:], 0.0)
            boards.append(board)

        warm_in = sb("warm_in", [P, 1], F32)
        warm_out = sb("warm_out", [P, 1], F32)
        nc.vector.memset(warm_in[:], 0.0)
        nc.scalar.activation(warm_out[:], warm_in[:], ACT.Sigmoid)
        load_plane(nc.gpsimd, w0_s, w0_scales)
        ident = sb("ident", [P, P], F32)
        make_identity(nc, ident[:])

        xo_w = load_words("xo_w", xo_words, U16, T)
        list2 = load_list("list2", offs2)
        load_plane(nc.sync, xo_s, xo_scales)
        w2_w = load_words("w2_w", w2_words, U32, R)
        xt_w = load_words("xt_w", xt_words, U32, T)
        load_plane(nc.sync, w2_s, w2_scales)
        w0_w = load_words("w0_w", w0_words, U32, R)
        list1 = load_list("list1", offs)
        load_plane(nc.sync, xt_s, xt_scales)
        w_w = load_words("w_w", w_words, U16, R)
        load_plane(nc.sync, w_s, w_scales)
        wb_w = load_words("wb_w", wb_words, U32, N)
        load_plane(nc.sync, wb_s, wb_scales)
        list3 = load_list("list3", offs3)
        wc_w = load_words("wc_w", wc_words, U16, N)
        load_plane(nc.sync, wc_s, wc_scales)
        list4 = load_list("list4", offs4)
        list5 = load_list("list5", offs5)
        list6 = load_list("list6", offs6)
        so_t = load_column("so_t", so)
        sp_t = load_column("sp_t", sp)
        bo_t = load_column("bo_t", bo)

        def gather(name, table, dtype, offsets):
            picked = sb(name, [P, 16 * offsets.shape[1]], dtype)
            nc.vector.tensor_copy(picked[:], table[:].indirect(offsets))
            return picked

        def half(lst, h):
            return lst[:, h * LIST_COLS : (h + 1) * LIST_COLS]

        a_ps = [bank("a%d" % h, "a%d" % h, [P, R]) for h in range(HALVES)]
        b_sb = []
        xo_g = []
        for h in range(HALVES):
            gs = gather("xo_gs%d" % h, xo_s, U8, half(list2, h))
            gw = gather("xo_gw%d" % h, xo_w, U16, half(list2, h))
            b_ps = bank("b%d" % h, "b%d" % h, [P, R])
            nc.tensor.matmul_mx(b_ps[:], gw[:].bitcast(E2M1), gs[:], w2_w[:].bitcast(E5M2), w2_s[:], start=True, stop=True)
            b_h = sb("b_sb%d" % h, [P, 2, P, 2], F32)
            nc.scalar.copy(b_h[:], b_ps[:].rearrange("j (p u e) -> j u p e", u=2, e=2))
            b_sb.append(b_h)
            xo_g.append((gw, gs))
        for h in range(HALVES):
            gw, gs = xo_g[h]
            nc.tensor.matmul_mx(a_ps[h][:], gw[:].bitcast(E2M1), gs[:], w0_w[:].bitcast(E5M2), w0_s[:], start=True, stop=False)
        for h in range(HALVES):
            gw = gather("xt_gw%d" % h, xt_w, U32, half(list1, h))
            gs = gather("xt_gs%d" % h, xt_s, U8, half(list1, h))
            nc.tensor.matmul_mx(
                a_ps[h][:], gw[:].bitcast(E4M3), gs[:], w_w[:].bitcast(E2M1), w_s[:],
                start=False, stop=True,
            )

        turned_ps = []
        for h in range(HALVES):
            turned = bank("turned%d" % h, "turned%d" % h, [P, 4, P])
            a_view = a_ps[h][:].rearrange("j (p u e) -> j u p e", u=2, e=2)
            for u in range(2):
                diff = sb("diff%d%d" % (h, u), [P, P, 2], F32)
                nc.vector.tensor_tensor(diff[:], a_view[:, u], b_sb[h][:, u], ALU.subtract)
                for e in range(2):
                    nc.tensor.transpose(turned[:, 2 * u + e, :], diff[:, :, e], ident[:])
            turned_ps.append(turned)

        hid_w = sb("hid_w", [P, J], U32)
        hid_s = sb("hid_s", [P, J], U8)
        for h in range(HALVES):
            turned = turned_ps[h]
            hid = sb("hid%d" % h, [P, P, 4], BF16)
            nc.scalar.activation(hid[:], turned[:].rearrange("p t j -> p j t"), ACT.Abs)
            cols = slice(h * P, (h + 1) * P)
            nc.vector.quantize_mx(hid_w[:, cols].bitcast(E4M3), hid_s[:, cols], hid[:].rearrange("p j t -> p (j t)"))
        for h in range(HALVES):
            cols = slice(h * P, (h + 1) * P)
            for n in reversed(range(TILES)):
                rows = slice(n * P, (n + 1) * P)
                p_ps = bank("p%d%d" % (h, n), ("p%d" if h == 0 else "b%d") % n, [P, P])
                nc.tensor.matmul_mx(
                    p_ps[:], wb_w[:, rows].bitcast(E5M2), wb_s[:, rows], hid_w[:, cols].bitcast(E4M3), hid_s[:, cols],
                    start=True, stop=True,
                )
                p_sb = sb("p_sb%d%d" % (h, n), [P, P], F32, "hid1" if h + n == 0 else "")
                places = boards[n][:].indirect(half(list3, h))
                if n == 0:
                    nc.vector.tensor_copy(p_sb[:], p_ps[:])
                    nc.vector.tensor_copy(places, p_sb[:])
                else:
                    nc.scalar.copy(p_sb[:], p_ps[:])
                    nc.scalar.activation(places, p_sb[:], ACT.Copy)

        q_ps = bank("q", "a0", [P, TILES, J])
        for n in range(TILES):
            rows = slice(n * P, (n + 1) * P)
            nc.tensor.matmul_mx(
                q_ps[:, n], wc_w[:, rows].bitcast(E2M1), wc_s[:, rows], hid_w[:].bitcast(E4M3), hid_s[:],
                start=True, stop=True,
            )
        q_sb = sb("q_sb", [P, TILES * J], F32)
        nc.vector.tensor_copy(q_sb[:], q_ps[:].rearrange("p n j -> p (n j)"))

        for n in reversed(range(TILES)):
            col = slice(n, n + 1)
            value = sb("value%d" % n, [P, O], F32)
            gate = sb("gate%d" % n, [P, O], F32)
            nc.scalar.activation(value[:], boards[n][:].indirect(list4[:]), ACT.Copy, scale=so_t[:, col])
            nc.scalar.activation(gate[:], boards[n][:].indirect(list5[:]), ACT.Sigmoid, bias=bo_t[:, col], scale=sp_t[:, col])
            taken = gather("taken%d" % n, q_sb[:, n * J : (n + 1) * J], F32, list6[:])
            gated = sb("gated%d" % n, [P, O], F32)
            multiplier = nc.gpsimd if n == 1 else nc.vector
            multiplier.tensor_tensor(gated[:], value[:], gate[:], ALU.mult)
            result = sb("result%d" % n, [P, O], F32)
            nc.vector.tensor_tensor(result[:], gated[:], taken[:], ALU.subtract)
            nc.sync.dma_start(out[n * P : (n + 1) * P, :], result[:])
